import numpy as np
import ml_dtypes


def mxq(x, axis, fmt="e4m3"):
    dtype, down = {"e4m3": (ml_dtypes.float8_e4m3fn, 7), "e5m2": (ml_dtypes.float8_e5m2, 14)}[fmt]
    v = np.moveaxis(np.asarray(x, np.float32).astype(ml_dtypes.bfloat16).astype(np.float64), axis, -1)
    blocks = v.reshape(v.shape[:-1] + (-1, 32))
    amax = np.abs(blocks).max(-1, keepdims=True)
    byte = np.maximum(np.where(amax > 0, np.frexp(amax)[1] - 1 + 127, 0) - down, 1)
    scale = np.exp2(byte - 127.0)
    codes = (blocks / scale).astype(np.float32).astype(dtype).astype(np.float64)
    return np.moveaxis((codes * scale).reshape(v.shape), -1, axis)


WIDE = False


def mx_kscale(k):
    if not WIDE:
        return np.ones(k)
    levels = np.array([30, -30])
    if k % 512:
        return np.exp2(np.random.permutation(np.resize(levels, k // 32))).repeat(32)
    a = np.empty((k // 512, 16))
    for p in range(k // 512):
        a[p, :8] = np.random.permutation(np.resize(levels, 8))
        for g in range(8):
            far = levels[np.abs(levels - a[p, g]) >= 10]
            a[p, g + 8] = far[np.random.randint(len(far))]
    return np.exp2(a.ravel()).repeat(32)


def f64(x):
    return np.asarray(x).astype(np.float64)


def striped(idx):
    return np.tile(np.asarray(idx).reshape(-1, 16).T, (8, 1)).astype(np.uint16)


def unstriped(offs):
    return offs[:16].T.reshape(-1).astype(np.int64)


def striped8(idx):
    return np.asarray(idx).reshape(8, -1, 16).transpose(0, 2, 1).reshape(128, -1).astype(np.uint16)


def unstriped8(offs):
    return offs.reshape(8, 16, -1).transpose(0, 2, 1).reshape(8, -1).astype(np.int64)


def pick8(x, idx, run):
    r = np.arange(len(x))
    return x[r[:, None], idx[r % (8 * run) // run]]


E2M1 = np.array([0.0, 0.5, 1.0, 1.5, 2.0, 3.0, 4.0, 6.0, -0.0, -0.5, -1.0, -1.5, -2.0, -3.0, -4.0, -6.0])


def pack_weight(w, fmt):
    k, n = w.shape
    w = f64(np.asarray(w, np.float32).astype(ml_dtypes.bfloat16)).reshape(k // 32, 32, n)
    amax = np.abs(w).max(1)
    if fmt in ("e4m3", "e5m2"):
        byte = np.frexp(amax)[1] - 1 + 127 - (7 if fmt == "e4m3" else 14)
    else:
        mant, ex = np.frexp(amax / 6.0)
        byte = np.where(mant > 0.5, ex, ex - 1) + 127
    byte = np.clip(np.where(amax > 0, byte, 1), 1, 254)
    scaled = (w * np.exp2(127.0 - byte)[:, None, :]).reshape(k, n).astype(np.float32)
    by_word = np.ascontiguousarray(scaled.reshape(k // 512, 128, 4, n).transpose(0, 1, 3, 2))
    if fmt in ("e4m3", "e5m2"):
        words = by_word.astype(ml_dtypes.float8_e4m3fn if fmt == "e4m3" else ml_dtypes.float8_e5m2).view(np.uint8)
    else:
        c = by_word.astype(ml_dtypes.float4_e2m1fn).view(np.uint8) & 0xF
        words = (c[..., 0::2] | (c[..., 1::2] << 4)).reshape(k // 512, 128, 2 * n)
    return np.ascontiguousarray(words), np.ascontiguousarray(byte.astype(np.uint8).reshape(k // 512, 16, n))


def unpack_weight(words, scales, fmt):
    g, _, n = scales.shape
    words = np.ascontiguousarray(words).reshape(g, 128, n, -1)
    if fmt in ("e4m3", "e5m2"):
        vals = words.view(ml_dtypes.float8_e4m3fn if fmt == "e4m3" else ml_dtypes.float8_e5m2).astype(np.float64)
    else:
        nib = np.empty((g, 128, n, 4), np.uint8)
        nib[..., 0::2] = words & 0xF
        nib[..., 1::2] = words >> 4
        vals = E2M1[nib]
    vals = vals * np.repeat(np.exp2(scales.astype(np.float64) - 127.0), 8, axis=1)[..., None]
    return vals.transpose(0, 1, 3, 2).reshape(g * 512, n)


K, T, J, R, F, Z, C, D, O, N, S = 512, 1024, 256, 512, 512, 1024, 512, 512, 128, 256, 1024


def setup_inputs():
    n = np.random.standard_normal
    idx = np.random.permutation(T)[:J]
    idx2 = np.random.permutation(Z)[:J]
    idx3 = np.stack([np.random.permutation(C)[:J] for _ in range(8)])
    idx4 = np.stack([np.random.permutation(D)[:J] for _ in range(8)])
    idx5 = np.random.permutation(C)[:O]
    idx6 = np.random.permutation(D)[:O]
    idx7 = np.random.permutation(S)[:N]
    fk = mx_kscale(K)
    ff = mx_kscale(F)
    fr = mx_kscale(R)
    xtp = pack_weight(n((K, T)) / fk[:, None], "e4m3")
    xop = pack_weight(n((F, Z)) / ff[:, None], "e2m1")
    wp = pack_weight(n((K, R)) * 1 / np.sqrt(K) * fk[:, None] * fr, "e2m1")
    w0p = pack_weight(n((F, R)) * 1 / np.sqrt(F) * ff[:, None] * fr, "e5m2")
    vsp = pack_weight(n((R, S)) * 1 / np.sqrt(R) / fr[:, None], "e5m2")
    return {
        "xt_words": xtp[0],
        "xt_scales": xtp[1],
        "xo_words": xop[0],
        "xo_scales": xop[1],
        "w_words": wp[0],
        "w_scales": wp[1],
        "w0_words": w0p[0],
        "w0_scales": w0p[1],
        "sa": (np.random.uniform(0.5, 1.6, (R, 1))).astype(np.float32),
        "sb": (np.random.uniform(0.5, 1.6, (R, 1))).astype(np.float32),
        "vs_words": vsp[0],
        "vs_scales": vsp[1],
        "offs": striped(idx),
        "offs2": striped(idx2),
        "offs3": striped8(idx3),
        "offs4": striped8(idx4),
        "offs5": striped(idx5),
        "offs6": striped(idx6),
        "offs7": striped(idx7),
    }


def reference(xt_words, xt_scales, xo_words, xo_scales, w_words, w_scales, w0_words, w0_scales, sa, sb, vs_words, vs_scales, offs, offs2, offs3, offs4, offs5, offs6, offs7):
    idx = unstriped(offs)
    idx2 = unstriped(offs2)
    idx3 = unstriped8(offs3)
    idx4 = unstriped8(offs4)
    idx5 = unstriped(offs5)
    idx6 = unstriped(offs6)
    idx7 = unstriped(offs7)
    xtu = unpack_weight(xt_words, xt_scales, "e4m3")
    xou = unpack_weight(xo_words, xo_scales, "e2m1")
    wu = unpack_weight(w_words, w_scales, "e2m1")
    w0u = unpack_weight(w0_words, w0_scales, "e5m2")
    vsu = unpack_weight(vs_words, vs_scales, "e5m2")
    xtidxg = xtu[:, idx]
    xoidx2g = xou[:, idx2]
    a = wu.T @ xtidxg + w0u.T @ xoidx2g
    pw = np.zeros((R, C))
    pw[np.arange(R)[:, None], idx3[np.arange(R) % 512 // 64]] = a
    pv = np.zeros((R, D))
    pv[np.arange(R)[:, None], idx4[np.arange(R) % 512 // 64]] = a
    hid = np.maximum(pw[:, idx5] * f64(sa), pv[:, idx6] * f64(sb))
    vsidx7g = vsu[:, idx7]
    hidq = mxq(hid, 0, "e4m3")
    y = vsidx7g.T @ hidq
    return y

@@ -1,0 +1,178 @@
+from contextlib import ExitStack
+
+import concourse.mybir as mybir
+
+FLOPS = 301989888
+
+F32 = mybir.dt.float32
+BF16 = mybir.dt.bfloat16
+I32 = mybir.dt.int32
+U32 = mybir.dt.uint32
+U16 = mybir.dt.uint16
+U8 = mybir.dt.uint8
+E4M3 = mybir.dt.float8_e4m3fn_x4
+E5M2 = mybir.dt.float8_e5m2_x4
+E2M1 = mybir.dt.float4_e2m1fn_x4
+COPY = mybir.ActivationFunctionType.Copy
+MAX = mybir.AluOpType.max
+
+P = 128
+PACK = 4
+J, R, BOARD, O, N = 256, 512, 512, 128, 256
+TABLE = 1024
+HALF = J // 2
+
+
+def tile_list_owntwice_bank_store_plain_kernel(
+    tc, xt_words, xt_scales, xo_words, xo_scales, w_words, w_scales, w0_words, w0_scales,
+    sa, sb, vs_words, vs_scales, offs, offs2, offs3, offs4, offs5, offs6, offs7, out,
+):
+    nc = tc.nc
+    with ExitStack() as ctx:
+        sbuf = ctx.enter_context(tc.tile_pool(name="sbuf", bufs=1))
+        psum = ctx.enter_context(tc.psum_pool(name="psum", bufs=1))
+
+        def new(name, shape, dtype):
+            return sbuf.tile(shape, dtype, name=name, align_bytes=64)
+
+        def load_list(name, src):
+            tile = sbuf.tile(list(src.shape), U16, name=name)
+            nc.sync.dma_start(tile[:], src)
+            return tile
+
+        def load_words(name, src, columns, dtype):
+            tile = new(name, [P, columns], dtype)
+            nc.sync.dma_start(tile[:].bitcast(I32), src.bitcast(I32))
+            return tile
+
+        def stage_scales(name, src, columns, engine):
+            stage = new(name, [64, 2, columns // 4], I32)
+            engine.memset(stage[:], 0)
+            rows = src[0].bitcast(I32).rearrange("(a b r) w -> b r a w", a=2, b=2)
+            for b in range(2):
+                nc.sync.dma_start(stage[32 * b : 32 * b + 4, :, :], rows[b])
+            return stage
+
+        def spread_scales(name, stage, columns):
+            plane = new(name, [P, columns], U8)
+            for a in range(2):
+                nc.vector.tensor_copy(plane[64 * a : 64 * a + 64, :].bitcast(I32), stage[:, a, :])
+            return plane
+
+        tok_list = load_list("tok_list", offs)
+        note_list = load_list("note_list", offs2)
+        xt_stage = stage_scales("xt_stage", xt_scales, TABLE, nc.vector)
+        xo_stage = stage_scales("xo_stage", xo_scales, TABLE, nc.vector)
+        xt_table = load_words("xt_table", xt_words[0].rearrange("p n t -> p (n t)"), TABLE, U32)
+        w_planes = new("w_planes", [P, 2, 2, R // 4], I32)
+        nc.vector.memset(w_planes[:], 0)
+        for which, src in enumerate((w_scales, w0_scales)):
+            rows = src[0].bitcast(I32).rearrange("(a b r) w -> b r a w", a=2, b=2)
+            for b in range(2):
+                nc.sync.dma_start(w_planes[32 * b : 32 * b + 4, :, which, :], rows[b])
+        xo_table = load_words("xo_table", xo_words[0], TABLE, U16)
+        w0_raw = load_words("w0_raw", w0_words[0].rearrange("p n t -> p (n t)"), R, U32)
+        w_raw = load_words("w_raw", w_words[0], R, U16)
+        pw_put = load_list("pw_put", offs3)
+        pv_put = load_list("pv_put", offs4)
+        pw_get = load_list("pw_get", offs5)
+        pv_get = load_list("pv_get", offs6)
+        sa_cols = new("sa_cols", [P, PACK], F32)
+        nc.sync.dma_start(sa_cols[:], sa.rearrange("(p t) o -> p (t o)", t=PACK))
+        sb_cols = new("sb_cols", [P, PACK], F32)
+        nc.sync.dma_start(sb_cols[:], sb.rearrange("(p t) o -> p (t o)", t=PACK))
+        store_list = load_list("store_list", offs7)
+        vs_stage = stage_scales("vs_stage", vs_scales, TABLE, nc.vector)
+        vs_table = load_words("vs_table", vs_words[0].rearrange("p n t -> p (n t)"), TABLE, U32)
+
+        pw = new("pw", [P, BOARD], F32)
+        pv = new("pv", [P, BOARD], F32)
+        nc.vector.memset(pw[:], 0.0)
+        nc.vector.memset(pv[:], 0.0)
+
+        xt_plane = spread_scales("xt_plane", xt_stage, TABLE)
+        xo_plane = spread_scales("xo_plane", xo_stage, TABLE)
+
+        xt_g = new("xt_g", [P, J], U32)
+        xt_gs = new("xt_gs", [P, J], U8)
+        xo_g = new("xo_g", [P, J], U16)
+        xo_gs = new("xo_gs", [P, J], U8)
+
+        def gather_slots(lo, hi):
+            cols = slice(lo // 16, hi // 16)
+            nc.vector.tensor_copy(xt_g[:, lo:hi], xt_table[:].indirect(tok_list[:, cols]))
+            nc.vector.tensor_copy(xo_g[:, lo:hi], xo_table[:].indirect(note_list[:, cols]))
+
+        def hidden(t, weights, lo, hi, copy):
+            w_t, ws_t, w0_t, w0s_t = weights
+            acc = psum.tile([P, hi - lo], F32, name="acc%d_%d" % (t, lo))
+            nc.tensor.matmul_mx(acc[:], lhsT=w_t.bitcast(E2M1), lhsT_scale=ws_t,
+                                rhs=xt_g[:, lo:hi].bitcast(E4M3), rhs_scale=xt_gs[:, lo:hi], start=True, stop=False)
+            nc.tensor.matmul_mx(acc[:], lhsT=w0_t.bitcast(E5M2), lhsT_scale=w0s_t,
+                                rhs=xo_g[:, lo:hi].bitcast(E2M1), rhs_scale=xo_gs[:, lo:hi], start=False, stop=True)
+            a_t = new("a%d_%d" % (t, lo), [P, hi - lo], F32)
+            copy(a_t[:], acc[:])
+            return a_t
+
+        def put(a_t, lo, hi):
+            cols = slice(lo // 16, hi // 16)
+            nc.scalar.activation(pw[:].indirect(pw_put[:, cols]), a_t[:], COPY)
+            nc.scalar.activation(pv[:].indirect(pv_put[:, cols]), a_t[:], COPY)
+
+        hid = new("hid", [P, O, PACK], BF16)
+
+        def fetch(t):
+            left = new("left%d" % t, [P, O], F32)
+            right = new("right%d" % t, [P, O], F32)
+            nc.scalar.activation(left[:], pw[:].indirect(pw_get[:]), COPY, scale=sa_cols[:, t : t + 1])
+            nc.scalar.activation(right[:], pv[:].indirect(pv_get[:]), COPY, scale=sb_cols[:, t : t + 1])
+            nc.vector.tensor_tensor(hid[:, :, t], left[:], right[:], MAX)
+
+        nc.vector.tensor_copy(xt_gs[:], xt_plane[:].indirect(tok_list[:]))
+        nc.vector.tensor_copy(xo_gs[:], xo_plane[:].indirect(note_list[:]))
+        nc.vector.tensor_copy(w_planes[64:128, 0, :, :], w_planes[0:64, 1, :, :])
+        w_bytes = w_planes[:, 0, :, :].rearrange("p i w -> p (i w)").bitcast(U8).rearrange("p (i m t) -> p t i m", i=2, t=PACK)
+
+        w0_dealt = new("w0_dealt", [P, PACK, P], U32)
+        nc.scalar.copy(w0_dealt[:], w0_raw[:].rearrange("p (m t) -> p t m", t=PACK))
+        w_first = new("w_first", [P, P], U16)
+        w_rest = new("w_rest", [P, PACK - 1, P], U16)
+        w_by_byte = w_raw[:].rearrange("p (m t) -> p t m", t=PACK)
+        nc.scalar.copy(w_first[:], w_by_byte[:, 0, :])
+        nc.scalar.copy(w_rest[:], w_by_byte[:, 1:, :])
+        w_dealt = [w_first[:]] + [w_rest[:, t, :] for t in range(PACK - 1)]
+
+        def weights_of(t):
+            scales = new("ws_t%d" % t, [P, 2, P], U8)
+            nc.vector.tensor_copy(scales[:], w_bytes[:, t, :, :])
+            return (w_dealt[t], scales[:, 0, :], w0_dealt[:, t, :], scales[:, 1, :])
+
+        first = weights_of(0)
+        gather_slots(0, HALF)
+        put(hidden(0, first, 0, HALF, nc.scalar.copy), 0, HALF)
+        gather_slots(HALF, J)
+        put(hidden(0, first, HALF, J, nc.vector.tensor_copy), HALF, J)
+        rest = [hidden(t, weights_of(t), 0, J, nc.vector.tensor_copy) for t in range(1, PACK)]
+        fetch(0)
+
+        vs_plane = spread_scales("vs_plane", vs_stage, TABLE)
+        vs_g = new("vs_g", [P, N], U32)
+        vs_gs = new("vs_gs", [P, N], U8)
+        nc.vector.tensor_copy(vs_gs[:], vs_plane[:].indirect(store_list[:]))
+        nc.vector.tensor_copy(vs_g[:], vs_table[:].indirect(store_list[:]))
+
+        for t in range(1, PACK):
+            put(rest[t - 1], 0, J)
+            fetch(t)
+
+        hid_q = new("hid_q", [P, O], U32)
+        hid_qs = new("hid_qs", [P, O], U8)
+        nc.vector.quantize_mx(hid_q[:].bitcast(E4M3), hid_qs[:], hid[:].rearrange("p o t -> p (o t)"))
+        for h, copy, queue in ((0, nc.vector.tensor_copy, nc.sync), (1, nc.scalar.copy, nc.scalar)):
+            rows = slice(P * h, P * (h + 1))
+            acc = psum.tile([P, O], F32, name="y%d" % h)
+            nc.tensor.matmul_mx(acc[:], lhsT=vs_g[:, rows].bitcast(E5M2), lhsT_scale=vs_gs[:, rows],
+                                rhs=hid_q[:].bitcast(E4M3), rhs_scale=hid_qs[:], start=True, stop=True)
+            res = new("res%d" % h, [P, O], F32)
+            copy(res[:], acc[:])
+            queue.dma_start(out[rows, :], res[:])

@@ -30,6 +30,7 @@ def tile_list_owntwice_bank_store_plain_kernel(
     nc = tc.nc
     with ExitStack() as ctx:
         sbuf = ctx.enter_context(tc.tile_pool(name="sbuf", bufs=1))
+        shared = ctx.enter_context(tc.tile_pool(name="shared", bufs=1))
         psum = ctx.enter_context(tc.psum_pool(name="psum", bufs=1))
 
         def new(name, shape, dtype):
@@ -45,32 +46,33 @@ def tile_list_owntwice_bank_store_plain_kernel(
             nc.sync.dma_start(tile[:].bitcast(I32), src.bitcast(I32))
             return tile
 
-        def stage_scales(name, src, columns, engine):
-            stage = new(name, [64, 2, columns // 4], I32)
-            engine.memset(stage[:], 0)
+        def load_scale_rows(stage, src):
             rows = src[0].bitcast(I32).rearrange("(a b r) w -> b r a w", a=2, b=2)
             for b in range(2):
-                nc.sync.dma_start(stage[32 * b : 32 * b + 4, :, :], rows[b])
+                nc.sync.dma_start(stage[32 * b : 32 * b + 4], rows[b])
+
+        def stage_scales(name, src):
+            stage = new(name, [64, 2, TABLE // 4], I32)
+            nc.vector.memset(stage[:], 0)
+            load_scale_rows(stage[:], src)
             return stage
 
-        def spread_scales(name, stage, columns):
-            plane = new(name, [P, columns], U8)
+        def spread_scales(name, stage):
+            plane = new(name, [P, TABLE], U8)
             for a in range(2):
                 nc.vector.tensor_copy(plane[64 * a : 64 * a + 64, :].bitcast(I32), stage[:, a, :])
             return plane
 
         tok_list = load_list("tok_list", offs)
         note_list = load_list("note_list", offs2)
-        xt_stage = stage_scales("xt_stage", xt_scales, TABLE, nc.vector)
-        xo_stage = stage_scales("xo_stage", xo_scales, TABLE, nc.vector)
+        xt_stage = stage_scales("xt_stage", xt_scales)
+        xo_stage = stage_scales("xo_stage", xo_scales)
         xt_table = load_words("xt_table", xt_words[0].rearrange("p n t -> p (n t)"), TABLE, U32)
-        w_planes = new("w_planes", [P, 2, 2, R // 4], I32)
-        nc.vector.memset(w_planes[:], 0)
-        for which, src in enumerate((w_scales, w0_scales)):
-            rows = src[0].bitcast(I32).rearrange("(a b r) w -> b r a w", a=2, b=2)
-            for b in range(2):
-                nc.sync.dma_start(w_planes[32 * b : 32 * b + 4, :, which, :], rows[b])
         xo_table = load_words("xo_table", xo_words[0], TABLE, U16)
+        w_stage = shared.tile([64, 2, 2 * R // 4], I32, name="w_stage", align_bytes=64, offset=0)
+        nc.vector.memset(w_stage[:], 0)
+        load_scale_rows(w_stage[:, :, : R // 4], w_scales)
+        load_scale_rows(w_stage[:, :, R // 4 :], w0_scales)
         w0_raw = load_words("w0_raw", w0_words[0].rearrange("p n t -> p (n t)"), R, U32)
         w_raw = load_words("w_raw", w_words[0], R, U16)
         pw_put = load_list("pw_put", offs3)
@@ -82,88 +84,115 @@ def tile_list_owntwice_bank_store_plain_kernel(
         sb_cols = new("sb_cols", [P, PACK], F32)
         nc.sync.dma_start(sb_cols[:], sb.rearrange("(p t) o -> p (t o)", t=PACK))
         store_list = load_list("store_list", offs7)
-        vs_stage = stage_scales("vs_stage", vs_scales, TABLE, nc.vector)
-        vs_table = load_words("vs_table", vs_words[0].rearrange("p n t -> p (n t)"), TABLE, U32)
-
         pw = new("pw", [P, BOARD], F32)
         pv = new("pv", [P, BOARD], F32)
         nc.vector.memset(pw[:], 0.0)
         nc.vector.memset(pv[:], 0.0)
+        vs_stage = stage_scales("vs_stage", vs_scales)
+        vs_table = load_words("vs_table", vs_words[0].rearrange("p n t -> p (n t)"), TABLE, U32)
 
-        xt_plane = spread_scales("xt_plane", xt_stage, TABLE)
-        xo_plane = spread_scales("xo_plane", xo_stage, TABLE)
+        xt_plane = spread_scales("xt_plane", xt_stage)
+        xo_plane = spread_scales("xo_plane", xo_stage)
 
-        xt_g = new("xt_g", [P, J], U32)
-        xt_gs = new("xt_gs", [P, J], U8)
-        xo_g = new("xo_g", [P, J], U16)
-        xo_gs = new("xo_gs", [P, J], U8)
+        def gather_slots(half, make):
+            cols = slice(half * HALF // 16, (half + 1) * HALF // 16)
+            picked = []
+            for name, window, entries, dtype, offset in (
+                ("xt_gs", xt_plane, tok_list, U8, 0),
+                ("xo_gs", xo_plane, note_list, U8, HALF),
+                ("xt_g", xt_table, tok_list, U32, 2 * HALF),
+                ("xo_g", xo_table, note_list, U16, 6 * HALF),
+            ):
+                tile = make(name + str(half), dtype, offset)
+                nc.vector.tensor_copy(tile[:], window[:].indirect(entries[:, cols]))
+                picked.append(tile)
+            return picked
 
-        def gather_slots(lo, hi):
-            cols = slice(lo // 16, hi // 16)
-            nc.vector.tensor_copy(xt_g[:, lo:hi], xt_table[:].indirect(tok_list[:, cols]))
-            nc.vector.tensor_copy(xo_g[:, lo:hi], xo_table[:].indirect(note_list[:, cols]))
+        first_half = gather_slots(0, lambda name, dtype, offset: new(name, [P, HALF], dtype))
+        w_plane = spread_scales("w_plane", w_stage)
+        w_bytes = w_plane[:].rearrange("p (i m t) -> p t i m", i=2, t=PACK)
 
-        def hidden(t, weights, lo, hi, copy):
-            w_t, ws_t, w0_t, w0s_t = weights
-            acc = psum.tile([P, hi - lo], F32, name="acc%d_%d" % (t, lo))
-            nc.tensor.matmul_mx(acc[:], lhsT=w_t.bitcast(E2M1), lhsT_scale=ws_t,
-                                rhs=xt_g[:, lo:hi].bitcast(E4M3), rhs_scale=xt_gs[:, lo:hi], start=True, stop=False)
-            nc.tensor.matmul_mx(acc[:], lhsT=w0_t.bitcast(E5M2), lhsT_scale=w0s_t,
-                                rhs=xo_g[:, lo:hi].bitcast(E2M1), rhs_scale=xo_gs[:, lo:hi], start=False, stop=True)
-            a_t = new("a%d_%d" % (t, lo), [P, hi - lo], F32)
-            copy(a_t[:], acc[:])
-            return a_t
+        def scales_of(t):
+            scales = new("ws%d" % t, [P, 2, P], U8)
+            nc.vector.tensor_copy(scales[:], w_bytes[:, t, :, :])
+            return scales
 
-        def put(a_t, lo, hi):
-            cols = slice(lo // 16, hi // 16)
+        def deal_first(name, raw, dtype):
+            dealt = new(name, [P, P], dtype)
+            nc.scalar.copy(dealt[:], raw[:, ::PACK])
+            return dealt
+
+        def deal_rest(name, raw, dtype, run, copy):
+            dealt = new(name, [P, PACK - 1, P], dtype)
+            copy(
+                dealt[:].rearrange("p t (c i) -> p c t i", i=run),
+                raw[:].rearrange("p (c i t) -> p c t i", i=run, t=PACK)[:, :, 1:, :],
+            )
+            return dealt
+
+        def multiply(acc, w_t, w0_t, scales, picked):
+            xt_gs, xo_gs, xt_g, xo_g = picked
+            nc.tensor.matmul_mx(acc, lhsT=w_t.bitcast(E2M1), lhsT_scale=scales[:, 0, :],
+                                rhs=xt_g[:].bitcast(E4M3), rhs_scale=xt_gs[:], start=True, stop=False)
+            nc.tensor.matmul_mx(acc, lhsT=w0_t.bitcast(E5M2), lhsT_scale=scales[:, 1, :],
+                                rhs=xo_g[:].bitcast(E2M1), rhs_scale=xo_gs[:], start=False, stop=True)
+
+        def put(a_t, cols):
             nc.scalar.activation(pw[:].indirect(pw_put[:, cols]), a_t[:], COPY)
             nc.scalar.activation(pv[:].indirect(pv_put[:, cols]), a_t[:], COPY)
 
-        hid = new("hid", [P, O, PACK], BF16)
-
-        def fetch(t):
+        def fetch(t, pieces):
             left = new("left%d" % t, [P, O], F32)
-            right = new("right%d" % t, [P, O], F32)
             nc.scalar.activation(left[:], pw[:].indirect(pw_get[:]), COPY, scale=sa_cols[:, t : t + 1])
-            nc.scalar.activation(right[:], pv[:].indirect(pv_get[:]), COPY, scale=sb_cols[:, t : t + 1])
-            nc.vector.tensor_tensor(hid[:, :, t], left[:], right[:], MAX)
+            width = O // pieces
+            for piece in range(pieces):
+                places = slice(piece * width, (piece + 1) * width)
+                entries = pv_get[:, piece * width // 16 : (piece + 1) * width // 16]
+                right = new("right%d_%d" % (t, piece), [P, width], F32)
+                nc.scalar.activation(right[:], pv[:].indirect(entries), COPY, scale=sb_cols[:, t : t + 1])
+                nc.vector.tensor_tensor(hid[:, places, t], left[:, places], right[:], MAX)
 
-        nc.vector.tensor_copy(xt_gs[:], xt_plane[:].indirect(tok_list[:]))
-        nc.vector.tensor_copy(xo_gs[:], xo_plane[:].indirect(note_list[:]))
-        nc.vector.tensor_copy(w_planes[64:128, 0, :, :], w_planes[0:64, 1, :, :])
-        w_bytes = w_planes[:, 0, :, :].rearrange("p i w -> p (i w)").bitcast(U8).rearrange("p (i m t) -> p t i m", i=2, t=PACK)
+        scales0 = scales_of(0)
+        w0_first = deal_first("w0_first", w0_raw, U32)
+        w_first = deal_first("w_first", w_raw, U16)
+        w0_rest = deal_rest("w0_rest", w0_raw, U32, 4, nc.scalar.copy)
 
-        w0_dealt = new("w0_dealt", [P, PACK, P], U32)
-        nc.scalar.copy(w0_dealt[:], w0_raw[:].rearrange("p (m t) -> p t m", t=PACK))
-        w_first = new("w_first", [P, P], U16)
-        w_rest = new("w_rest", [P, PACK - 1, P], U16)
-        w_by_byte = w_raw[:].rearrange("p (m t) -> p t m", t=PACK)
-        nc.scalar.copy(w_first[:], w_by_byte[:, 0, :])
-        nc.scalar.copy(w_rest[:], w_by_byte[:, 1:, :])
-        w_dealt = [w_first[:]] + [w_rest[:, t, :] for t in range(PACK - 1)]
+        def first_rows(half, picked, copy):
+            acc = psum.tile([P, HALF], F32, name="acc", tag="bank%d" % half)
+            multiply(acc[:], w_first[:], w0_first[:], scales0, picked)
+            a_half = new("a0_%d" % half, [P, HALF], F32)
+            copy(a_half[:], acc[:])
+            put(a_half, slice(half * HALF // 16, (half + 1) * HALF // 16))
 
-        def weights_of(t):
-            scales = new("ws_t%d" % t, [P, 2, P], U8)
-            nc.vector.tensor_copy(scales[:], w_bytes[:, t, :, :])
-            return (w_dealt[t], scales[:, 0, :], w0_dealt[:, t, :], scales[:, 1, :])
+        first_rows(0, first_half, nc.scalar.copy)
+        second_half = gather_slots(
+            1, lambda name, dtype, offset: shared.tile([P, HALF], dtype, name=name, align_bytes=64, offset=offset)
+        )
+        first_rows(1, second_half, nc.vector.tensor_copy)
 
-        first = weights_of(0)
-        gather_slots(0, HALF)
-        put(hidden(0, first, 0, HALF, nc.scalar.copy), 0, HALF)
-        gather_slots(HALF, J)
-        put(hidden(0, first, HALF, J, nc.vector.tensor_copy), HALF, J)
-        rest = [hidden(t, weights_of(t), 0, J, nc.vector.tensor_copy) for t in range(1, PACK)]
-        fetch(0)
+        w_rest = deal_rest("w_rest", w_raw, U16, 8, nc.vector.tensor_copy)
+        rest = []
+        for t in range(1, PACK):
+            scales = scales_of(t)
+            acc = psum.tile([P, 2, HALF], F32, name="acc", tag="bank%d" % ((t - 1) % 2))
+            for half, picked in enumerate((first_half, second_half)):
+                multiply(acc[:, half, :], w_rest[:, t - 1, :], w0_rest[:, t - 1, :], scales, picked)
+            a_t = new("a%d" % t, [P, J], F32)
+            nc.vector.tensor_copy(a_t[:], acc[:].rearrange("p h j -> p (h j)"))
+            rest.append(a_t)
 
-        vs_plane = spread_scales("vs_plane", vs_stage, TABLE)
+        vs_plane = spread_scales("vs_plane", vs_stage)
         vs_g = new("vs_g", [P, N], U32)
         vs_gs = new("vs_gs", [P, N], U8)
         nc.vector.tensor_copy(vs_gs[:], vs_plane[:].indirect(store_list[:]))
         nc.vector.tensor_copy(vs_g[:], vs_table[:].indirect(store_list[:]))
 
+        hid = sbuf.tile([P, O, PACK], BF16, name="hid", tag="vs_table", align_bytes=64)
+        fetch(0, 1)
+
         for t in range(1, PACK):
-            put(rest[t - 1], 0, J)
-            fetch(t)
+            put(rest[t - 1], slice(0, J // 16))
+            fetch(t, 2 if t == PACK - 1 else 1)
 
         hid_q = new("hid_q", [P, O], U32)
         hid_qs = new("hid_qs", [P, O], U8)

@@ -51,8 +51,8 @@ def tile_list_owntwice_bank_store_plain_kernel(
             for b in range(2):
                 nc.sync.dma_start(stage[32 * b : 32 * b + 4], rows[b])
 
-        def stage_scales(name, src):
-            stage = new(name, [64, 2, TABLE // 4], I32)
+        def stage_scales(name, src, tag):
+            stage = sbuf.tile([64, 2, TABLE // 4], I32, name=name, tag=tag, align_bytes=64)
             nc.vector.memset(stage[:], 0)
             load_scale_rows(stage[:], src)
             return stage
@@ -65,8 +65,8 @@ def tile_list_owntwice_bank_store_plain_kernel(
 
         tok_list = load_list("tok_list", offs)
         note_list = load_list("note_list", offs2)
-        xt_stage = stage_scales("xt_stage", xt_scales)
-        xo_stage = stage_scales("xo_stage", xo_scales)
+        xt_stage = stage_scales("xt_stage", xt_scales, "xt_stage")
+        xo_stage = stage_scales("xo_stage", xo_scales, "xo_stage")
         xt_table = load_words("xt_table", xt_words[0].rearrange("p n t -> p (n t)"), TABLE, U32)
         xo_table = load_words("xo_table", xo_words[0], TABLE, U16)
         w_stage = shared.tile([64, 2, 2 * R // 4], I32, name="w_stage", align_bytes=64, offset=0)
@@ -85,14 +85,13 @@ def tile_list_owntwice_bank_store_plain_kernel(
         nc.sync.dma_start(sb_cols[:], sb.rearrange("(p t) o -> p (t o)", t=PACK))
         store_list = load_list("store_list", offs7)
         pw = new("pw", [P, BOARD], F32)
-        pv = new("pv", [P, BOARD], F32)
         nc.vector.memset(pw[:], 0.0)
-        nc.vector.memset(pv[:], 0.0)
-        vs_stage = stage_scales("vs_stage", vs_scales)
         vs_table = load_words("vs_table", vs_words[0].rearrange("p n t -> p (n t)"), TABLE, U32)
 
         xt_plane = spread_scales("xt_plane", xt_stage)
         xo_plane = spread_scales("xo_plane", xo_stage)
+        pv = sbuf.tile([P, BOARD], F32, name="pv", tag="xo_stage", align_bytes=64)
+        nc.gpsimd.memset(pv[:], 0.0)
 
         def gather_slots(half, make):
             cols = slice(half * HALF // 16, (half + 1) * HALF // 16)
@@ -181,7 +180,7 @@ def tile_list_owntwice_bank_store_plain_kernel(
             nc.vector.tensor_copy(a_t[:], acc[:].rearrange("p h j -> p (h j)"))
             rest.append(a_t)
 
-        vs_plane = spread_scales("vs_plane", vs_stage)
+        vs_plane = spread_scales("vs_plane", stage_scales("vs_stage", vs_scales, "xo_table"))
         vs_g = new("vs_g", [P, N], U32)
         vs_gs = new("vs_gs", [P, N], U8)
         nc.vector.tensor_copy(vs_gs[:], vs_plane[:].indirect(store_list[:]))

from contextlib import ExitStack

import concourse.mybir as mybir

FLOPS = 301989888

F32 = mybir.dt.float32
BF16 = mybir.dt.bfloat16
I32 = mybir.dt.int32
U32 = mybir.dt.uint32
U16 = mybir.dt.uint16
U8 = mybir.dt.uint8
E4M3 = mybir.dt.float8_e4m3fn_x4
E5M2 = mybir.dt.float8_e5m2_x4
E2M1 = mybir.dt.float4_e2m1fn_x4
COPY = mybir.ActivationFunctionType.Copy
MAX = mybir.AluOpType.max

P = 128
PACK = 4
J, R, BOARD, O, N = 256, 512, 512, 128, 256
TABLE = 1024
HALF = J // 2


def tile_list_owntwice_bank_store_plain_kernel(
    tc, xt_words, xt_scales, xo_words, xo_scales, w_words, w_scales, w0_words, w0_scales,
    sa, sb, vs_words, vs_scales, offs, offs2, offs3, offs4, offs5, offs6, offs7, out,
):
    nc = tc.nc
    with ExitStack() as ctx:
        sbuf = ctx.enter_context(tc.tile_pool(name="sbuf", bufs=1))
        shared = ctx.enter_context(tc.tile_pool(name="shared", bufs=1))
        psum = ctx.enter_context(tc.psum_pool(name="psum", bufs=1))

        def new(name, shape, dtype):
            return sbuf.tile(shape, dtype, name=name, align_bytes=64)

        def load_list(name, src):
            tile = sbuf.tile(list(src.shape), U16, name=name)
            nc.sync.dma_start(tile[:], src)
            return tile

        def load_words(name, src, columns, dtype):
            tile = new(name, [P, columns], dtype)
            nc.sync.dma_start(tile[:].bitcast(I32), src.bitcast(I32))
            return tile

        def load_scale_rows(stage, src):
            rows = src[0].bitcast(I32).rearrange("(a b r) w -> b r a w", a=2, b=2)
            for b in range(2):
                nc.sync.dma_start(stage[32 * b : 32 * b + 4], rows[b])

        def stage_scales(name, src, tag):
            stage = sbuf.tile([64, 2, TABLE // 4], I32, name=name, tag=tag, align_bytes=64)
            nc.vector.memset(stage[:], 0)
            load_scale_rows(stage[:], src)
            return stage

        def spread_scales(name, stage):
            plane = new(name, [P, TABLE], U8)
            for a in range(2):
                nc.vector.tensor_copy(plane[64 * a : 64 * a + 64, :].bitcast(I32), stage[:, a, :])
            return plane

        tok_list = load_list("tok_list", offs)
        note_list = load_list("note_list", offs2)
        xt_stage = stage_scales("xt_stage", xt_scales, "xt_stage")
        xo_stage = stage_scales("xo_stage", xo_scales, "xo_stage")
        xt_table = load_words("xt_table", xt_words[0].rearrange("p n t -> p (n t)"), TABLE, U32)
        xo_table = load_words("xo_table", xo_words[0], TABLE, U16)
        w_stage = shared.tile([64, 2, 2 * R // 4], I32, name="w_stage", align_bytes=64, offset=0)
        nc.vector.memset(w_stage[:], 0)
        load_scale_rows(w_stage[:, :, : R // 4], w_scales)
        load_scale_rows(w_stage[:, :, R // 4 :], w0_scales)
        w0_raw = load_words("w0_raw", w0_words[0].rearrange("p n t -> p (n t)"), R, U32)
        w_raw = load_words("w_raw", w_words[0], R, U16)
        pw_put = load_list("pw_put", offs3)
        pv_put = load_list("pv_put", offs4)
        pw_get = load_list("pw_get", offs5)
        pv_get = load_list("pv_get", offs6)
        sa_cols = new("sa_cols", [P, PACK], F32)
        nc.sync.dma_start(sa_cols[:], sa.rearrange("(p t) o -> p (t o)", t=PACK))
        sb_cols = new("sb_cols", [P, PACK], F32)
        nc.sync.dma_start(sb_cols[:], sb.rearrange("(p t) o -> p (t o)", t=PACK))
        store_list = load_list("store_list", offs7)
        pw = new("pw", [P, BOARD], F32)
        nc.vector.memset(pw[:], 0.0)
        vs_table = load_words("vs_table", vs_words[0].rearrange("p n t -> p (n t)"), TABLE, U32)

        xt_plane = spread_scales("xt_plane", xt_stage)
        xo_plane = spread_scales("xo_plane", xo_stage)
        pv = sbuf.tile([P, BOARD], F32, name="pv", tag="xo_stage", align_bytes=64)
        nc.gpsimd.memset(pv[:], 0.0)

        def gather_slots(half, make):
            cols = slice(half * HALF // 16, (half + 1) * HALF // 16)
            picked = []
            for name, window, entries, dtype, offset in (
                ("xt_gs", xt_plane, tok_list, U8, 0),
                ("xo_gs", xo_plane, note_list, U8, HALF),
                ("xt_g", xt_table, tok_list, U32, 2 * HALF),
                ("xo_g", xo_table, note_list, U16, 6 * HALF),
            ):
                tile = make(name + str(half), dtype, offset)
                nc.vector.tensor_copy(tile[:], window[:].indirect(entries[:, cols]))
                picked.append(tile)
            return picked

        first_half = gather_slots(0, lambda name, dtype, offset: new(name, [P, HALF], dtype))
        w_plane = spread_scales("w_plane", w_stage)
        w_bytes = w_plane[:].rearrange("p (i m t) -> p t i m", i=2, t=PACK)

        def scales_of(t):
            scales = new("ws%d" % t, [P, 2, P], U8)
            nc.vector.tensor_copy(scales[:], w_bytes[:, t, :, :])
            return scales

        def deal_first(name, raw, dtype):
            dealt = new(name, [P, P], dtype)
            nc.scalar.copy(dealt[:], raw[:, ::PACK])
            return dealt

        def deal_rest(name, raw, dtype, run, copy):
            dealt = new(name, [P, PACK - 1, P], dtype)
            copy(
                dealt[:].rearrange("p t (c i) -> p c t i", i=run),
                raw[:].rearrange("p (c i t) -> p c t i", i=run, t=PACK)[:, :, 1:, :],
            )
            return dealt

        def multiply(acc, w_t, w0_t, scales, picked):
            xt_gs, xo_gs, xt_g, xo_g = picked
            nc.tensor.matmul_mx(acc, lhsT=w_t.bitcast(E2M1), lhsT_scale=scales[:, 0, :],
                                rhs=xt_g[:].bitcast(E4M3), rhs_scale=xt_gs[:], start=True, stop=False)
            nc.tensor.matmul_mx(acc, lhsT=w0_t.bitcast(E5M2), lhsT_scale=scales[:, 1, :],
                                rhs=xo_g[:].bitcast(E2M1), rhs_scale=xo_gs[:], start=False, stop=True)

        def put(a_t, cols):
            nc.scalar.activation(pw[:].indirect(pw_put[:, cols]), a_t[:], COPY)
            nc.scalar.activation(pv[:].indirect(pv_put[:, cols]), a_t[:], COPY)

        def fetch(t, pieces):
            left = new("left%d" % t, [P, O], F32)
            nc.scalar.activation(left[:], pw[:].indirect(pw_get[:]), COPY, scale=sa_cols[:, t : t + 1])
            width = O // pieces
            for piece in range(pieces):
                places = slice(piece * width, (piece + 1) * width)
                entries = pv_get[:, piece * width // 16 : (piece + 1) * width // 16]
                right = new("right%d_%d" % (t, piece), [P, width], F32)
                nc.scalar.activation(right[:], pv[:].indirect(entries), COPY, scale=sb_cols[:, t : t + 1])
                nc.vector.tensor_tensor(hid[:, places, t], left[:, places], right[:], MAX)

        scales0 = scales_of(0)
        w0_first = deal_first("w0_first", w0_raw, U32)
        w_first = deal_first("w_first", w_raw, U16)
        w0_rest = deal_rest("w0_rest", w0_raw, U32, 4, nc.scalar.copy)

        def first_rows(half, picked, copy):
            acc = psum.tile([P, HALF], F32, name="acc", tag="bank%d" % half)
            multiply(acc[:], w_first[:], w0_first[:], scales0, picked)
            a_half = new("a0_%d" % half, [P, HALF], F32)
            copy(a_half[:], acc[:])
            put(a_half, slice(half * HALF // 16, (half + 1) * HALF // 16))

        first_rows(0, first_half, nc.scalar.copy)
        second_half = gather_slots(
            1, lambda name, dtype, offset: shared.tile([P, HALF], dtype, name=name, align_bytes=64, offset=offset)
        )
        first_rows(1, second_half, nc.vector.tensor_copy)

        w_rest = deal_rest("w_rest", w_raw, U16, 8, nc.vector.tensor_copy)
        rest = []
        for t in range(1, PACK):
            scales = scales_of(t)
            acc = psum.tile([P, 2, HALF], F32, name="acc", tag="bank%d" % ((t - 1) % 2))
            for half, picked in enumerate((first_half, second_half)):
                multiply(acc[:, half, :], w_rest[:, t - 1, :], w0_rest[:, t - 1, :], scales, picked)
            a_t = new("a%d" % t, [P, J], F32)
            nc.vector.tensor_copy(a_t[:], acc[:].rearrange("p h j -> p (h j)"))
            rest.append(a_t)

        vs_plane = spread_scales("vs_plane", stage_scales("vs_stage", vs_scales, "xo_table"))
        vs_g = new("vs_g", [P, N], U32)
        vs_gs = new("vs_gs", [P, N], U8)
        nc.vector.tensor_copy(vs_gs[:], vs_plane[:].indirect(store_list[:]))
        nc.vector.tensor_copy(vs_g[:], vs_table[:].indirect(store_list[:]))

        hid = sbuf.tile([P, O, PACK], BF16, name="hid", tag="vs_table", align_bytes=64)
        fetch(0, 1)

        for t in range(1, PACK):
            put(rest[t - 1], slice(0, J // 16))
            fetch(t, 2 if t == PACK - 1 else 1)

        hid_q = new("hid_q", [P, O], U32)
        hid_qs = new("hid_qs", [P, O], U8)
        nc.vector.quantize_mx(hid_q[:].bitcast(E4M3), hid_qs[:], hid[:].rearrange("p o t -> p (o t)"))
        for h, copy, queue in ((0, nc.vector.tensor_copy, nc.sync), (1, nc.scalar.copy, nc.scalar)):
            rows = slice(P * h, P * (h + 1))
            acc = psum.tile([P, O], F32, name="y%d" % h)
            nc.tensor.matmul_mx(acc[:], lhsT=vs_g[:, rows].bitcast(E5M2), lhsT_scale=vs_gs[:, rows],
                                rhs=hid_q[:].bitcast(E4M3), rhs_scale=hid_qs[:], start=True, stop=True)
            res = new("res%d" % h, [P, O], F32)
            copy(res[:], acc[:])
            queue.dma_start(out[rows, :], res[:])
